import numpy as np
import ml_dtypes


def mxq(x, axis, fmt="e4m3"):
    dtype, down = {"e4m3": (ml_dtypes.float8_e4m3fn, 7), "e5m2": (ml_dtypes.float8_e5m2, 14)}[fmt]
    v = np.moveaxis(np.asarray(x, np.float32).astype(ml_dtypes.bfloat16).astype(np.float64), axis, -1)
    blocks = v.reshape(v.shape[:-1] + (-1, 32))
    amax = np.abs(blocks).max(-1, keepdims=True)
    byte = np.maximum(np.where(amax > 0, np.frexp(amax)[1] - 1 + 127, 0) - down, 1)
    scale = np.exp2(byte - 127.0)
    codes = (blocks / scale).astype(np.float32).astype(dtype).astype(np.float64)
    return np.moveaxis((codes * scale).reshape(v.shape), -1, axis)


WIDE = False


def mx_kscale(k):
    if not WIDE:
        return np.ones(k)
    levels = np.array([10, -10, 5, -5, 0])
    if k % 512:
        return np.exp2(np.random.permutation(np.resize(levels, k // 32))).repeat(32)
    a = np.empty((k // 512, 16))
    for p in range(k // 512):
        a[p, :8] = np.random.permutation(np.resize(levels, 8))
        for g in range(8):
            far = levels[np.abs(levels - a[p, g]) >= 10]
            a[p, g + 8] = far[np.random.randint(len(far))]
    return np.exp2(a.ravel()).repeat(32)


def f64(x):
    return np.asarray(x).astype(np.float64)


def striped(idx):
    return np.tile(np.asarray(idx).reshape(-1, 16).T, (8, 1)).astype(np.uint16)


def unstriped(offs):
    return offs[:16].T.reshape(-1).astype(np.int64)


E2M1 = np.array([0.0, 0.5, 1.0, 1.5, 2.0, 3.0, 4.0, 6.0, -0.0, -0.5, -1.0, -1.5, -2.0, -3.0, -4.0, -6.0])


def pack_weight(w, fmt):
    k, n = w.shape
    w = f64(np.asarray(w, np.float32).astype(ml_dtypes.bfloat16)).reshape(k // 32, 32, n)
    amax = np.abs(w).max(1)
    if fmt == "e4m3":
        byte = np.frexp(amax)[1] - 1 + 127 - 7
    else:
        mant, ex = np.frexp(amax / 6.0)
        byte = np.where(mant > 0.5, ex, ex - 1) + 127
    byte = np.clip(np.where(amax > 0, byte, 1), 1, 254)
    scaled = (w * np.exp2(127.0 - byte)[:, None, :]).reshape(k, n).astype(np.float32)
    by_word = np.ascontiguousarray(scaled.reshape(k // 512, 128, 4, n).transpose(0, 1, 3, 2))
    if fmt == "e4m3":
        words = by_word.astype(ml_dtypes.float8_e4m3fn).view(np.uint8)
    else:
        c = by_word.astype(ml_dtypes.float4_e2m1fn).view(np.uint8) & 0xF
        words = (c[..., 0::2] | (c[..., 1::2] << 4)).reshape(k // 512, 128, 2 * n)
    return np.ascontiguousarray(words), np.ascontiguousarray(byte.astype(np.uint8).reshape(k // 512, 16, n))


def unpack_weight(words, scales, fmt):
    g, _, n = scales.shape
    words = np.ascontiguousarray(words).reshape(g, 128, n, -1)
    if fmt == "e4m3":
        vals = words.view(ml_dtypes.float8_e4m3fn).astype(np.float64)
    else:
        nib = np.empty((g, 128, n, 4), np.uint8)
        nib[..., 0::2] = words & 0xF
        nib[..., 1::2] = words >> 4
        vals = E2M1[nib]
    vals = vals * np.repeat(np.exp2(scales.astype(np.float64) - 127.0), 8, axis=1)[..., None]
    return vals.transpose(0, 1, 3, 2).reshape(g * 512, n)


def bf(x):
    return np.asarray(x, np.float32).astype(ml_dtypes.bfloat16)


def planes(Y):
    r, m = Y.shape
    b = f64(bf(Y)).reshape(r // 32, 32, m)
    amax = np.abs(b).max(1)
    byte = np.clip(np.where(amax > 0, np.frexp(amax)[1] - 1 + 127 - 7, 1), 1, 254)
    codes = (b * np.exp2(127.0 - byte)[:, None, :]).reshape(r, m).astype(np.float32).astype(ml_dtypes.float8_e4m3fn).view(np.uint8)
    words = codes.reshape(r // 512, 128, 4, m).transpose(0, 1, 3, 2)
    return np.ascontiguousarray(words), np.ascontiguousarray(byte.astype(np.uint8).reshape(r // 512, 16, m))


K, T, J, B, N = 1024, 2048, 512, 64, 512


def setup_inputs():
    n = np.random.standard_normal
    idx = np.random.permutation(T)[:J]
    fk = mx_kscale(K)
    wp = pack_weight(n((K, N)) * 1 / np.sqrt(K) * fk[:, None], "e2m1")
    return {
        "xt": (n((K, T)) / fk[:, None]).astype(np.float32),
        "w_words": wp[0],
        "w_scales": wp[1],
        "offs": striped(idx),
    }


def reference(xt, w_words, w_scales, offs):
    idx = unstriped(offs)
    wu = unpack_weight(w_words, w_scales, "e2m1")
    xtidxq = mxq(f64(xt)[:, idx], 0, "e4m3")
    z = wu.T @ xtidxq
    r1 = z.reshape(N, B, J // B).max(axis=2) + (0.0 - z).reshape(N, B, J // B).max(axis=2)
    m1 = z.reshape(N, B, J // B).mean(axis=2)
    y = r1 / (1.0 + np.abs(m1))
    words, scales = planes(y)
    return y, words, scales

@@ -1,0 +1,170 @@
+from contextlib import ExitStack
+
+import concourse.mybir as mybir
+from concourse.masks import make_identity
+
+K, T, J, B, N = 1024, 2048, 512, 64, 512
+FLOPS = 2 * K * J * N
+
+F32 = mybir.dt.float32
+BF16 = mybir.dt.bfloat16
+I32 = mybir.dt.int32
+U32 = mybir.dt.uint32
+U16 = mybir.dt.uint16
+U8 = mybir.dt.uint8
+FP8X4 = mybir.dt.float8_e4m3fn_x4
+FP4X4 = mybir.dt.float4_e2m1fn_x4
+ALU = mybir.AluOpType
+ACT = mybir.ActivationFunctionType
+
+P = 128
+PACK = 4
+PASSES = K // (P * PACK)
+GROUP = J // B
+HALVES = 2
+JH = J // HALVES
+BH = B // HALVES
+NMM = 128
+PAIRS = 2
+TP = PACK // PAIRS
+
+
+def tile_list_range_of_picked_groups_pl_kernel(tc, xt, w_words, w_scales, offs, out_0, out_1, out_2):
+    nc = tc.nc
+    with ExitStack() as ctx:
+        sb = ctx.enter_context(tc.tile_pool(name="sb", bufs=1))
+        ps = ctx.enter_context(tc.psum_pool(name="ps", bufs=1))
+
+        offsets = sb.tile([P, J // 16], U16, name="offsets")
+        w_raw = sb.tile([P, PASSES, 2 * N], U8, name="w_raw")
+        ws_raw = sb.tile([P, PASSES, N], U8, name="ws_raw")
+        nc.vector.memset(ws_raw[:].bitcast(I32), 0)
+        nc.sync.dma_start(out=w_raw[:].bitcast(I32), in_=w_words.rearrange("a p c -> p a c").bitcast(I32))
+        nc.sync.dma_start(offsets[:], offs)
+        for q in range(4):
+            nc.scalar.dma_start(
+                out=ws_raw[32 * q : 32 * q + 4, :, :].bitcast(I32),
+                in_=w_scales[:, 4 * q : 4 * q + 4, :].rearrange("a r c -> r a c").bitcast(I32),
+            )
+        rows = xt.rearrange("(a p t) c -> a t p c", a=PASSES, t=PACK)
+        planes = {}
+        for a in range(PASSES):
+            for t in range(PACK):
+                planes[a, t] = sb.tile([P, T], F32, name="plane_%d_%d" % (a, t))
+                nc.sync.dma_start(out=planes[a, t][:], in_=rows[a, t])
+
+        one = sb.tile([P, 1], F32, name="one")
+        nc.gpsimd.memset(one[:], 1.0)
+        warm = sb.tile([P, 1], F32, name="warm")
+        nc.scalar.activation(out=warm[:], in_=one[:], func=ACT.Abs_reciprocal_sqrt, bias=one[:])
+        ident = sb.tile([P, P], F32, name="ident")
+        make_identity(nc, ident[:])
+
+        w_dealt = sb.tile([P, PASSES * PACK, 2 * P], U8, name="w_dealt", align_bytes=64)
+        ws_dealt = sb.tile([P, PASSES * PACK, P], U8, name="ws_dealt", align_bytes=64)
+        nc.vector.tensor_copy(
+            out=w_dealt[:].rearrange("p (a t) (q two) -> p a t q two", t=PACK, two=2),
+            in_=w_raw[:].rearrange("p a (q t two) -> p a t q two", t=PACK, two=2),
+        )
+        nc.vector.tensor_copy(
+            out=ws_dealt[:].rearrange("p (a t) q -> p a t q", t=PACK),
+            in_=ws_raw[:].rearrange("p a (q t) -> p a t q", t=PACK),
+        )
+
+        banks = {}
+        for h in range(HALVES):
+            for u in range(PAIRS):
+                banks[h, u] = ps.tile([P, TP, JH], F32, name="z_%d_%d" % (h, u))
+
+        def gather(a, t, h, picked):
+            nc.vector.tensor_copy(
+                out=picked[:, :, t],
+                in_=planes[a, t][:].indirect(offsets[:, h * (JH // 16) : (h + 1) * (JH // 16)]),
+            )
+
+        def multiply(a, h, picked):
+            codes = sb.tile([P, JH], U32, name="codes_%d_%d" % (a, h), align_bytes=64)
+            scales = sb.tile([P, JH], U8, name="scales_%d_%d" % (a, h), align_bytes=64)
+            nc.vector.quantize_mx(out=codes[:].bitcast(FP8X4), scales=scales[:], in_=picked[:].rearrange("p j t -> p (j t)"))
+            for u in range(PAIRS):
+                for t2 in range(TP):
+                    s = a * PACK + u * TP + t2
+                    for c in range(JH // NMM):
+                        cols = slice(c * NMM, (c + 1) * NMM)
+                        nc.tensor.matmul_mx(
+                            out=banks[h, u][:, t2, cols],
+                            lhsT=w_dealt[:, s, :].bitcast(FP4X4),
+                            lhsT_scale=ws_dealt[:, s, :],
+                            rhs=codes[:, cols].bitcast(FP8X4),
+                            rhs_scale=scales[:, cols],
+                            start=(a == 0 and t2 == 0 and c == 0),
+                            stop=(a == PASSES - 1 and t2 == TP - 1 and c == JH // NMM - 1),
+                        )
+
+        for a in range(PASSES):
+            picked = [sb.tile([P, JH, PACK], BF16, name="picked_%d_%d" % (a, h), align_bytes=64) for h in range(HALVES)]
+            for t in range(PACK):
+                for h in range(HALVES):
+                    gather(a, t, h, picked[h])
+                    if t == PACK - 1:
+                        multiply(a, h, picked[h])
+
+        W = PACK * BH
+        hi4 = sb.tile([P, HALVES, 4, W], F32, name="hi4")
+        lo4 = sb.tile([P, HALVES, 4, W], F32, name="lo4")
+        hi2 = sb.tile([P, HALVES, 2, W], F32, name="hi2")
+        lo2 = sb.tile([P, HALVES, 2, W], F32, name="lo2")
+        inv = ps.tile([P, HALVES, W], F32, name="inv")
+        for h in range(HALVES):
+            z = sb.tile([P, GROUP, W], F32, name="zs_%d" % h)
+            for u in range(PAIRS):
+                cols = slice(u * TP * BH, (u + 1) * TP * BH)
+                nc.scalar.copy(
+                    out=z[:, :, cols].rearrange("p i (t b) -> p i t b", t=TP),
+                    in_=banks[h, u][:].rearrange("p t (b i) -> p i t b", i=GROUP),
+                )
+                nc.vector.tensor_tensor(out=hi4[:, h, :, cols], in0=z[:, 0:4, cols], in1=z[:, 4:8, cols], op=ALU.max)
+                nc.vector.tensor_tensor(out=lo4[:, h, :, cols], in0=z[:, 0:4, cols], in1=z[:, 4:8, cols], op=ALU.min)
+            nc.vector.tensor_tensor(out=hi2[:, h], in0=hi4[:, h, 0:2, :], in1=hi4[:, h, 2:4, :], op=ALU.max)
+            nc.vector.tensor_tensor(out=lo2[:, h], in0=lo4[:, h, 0:2, :], in1=lo4[:, h, 2:4, :], op=ALU.min)
+            sums = ps.tile([P, P], F32, name="sums_%d" % h)
+            for i in range(GROUP):
+                nc.tensor.matmul(sums[:], lhsT=z[:, i, :], rhs=ident[:], start=(i == 0), stop=(i == GROUP - 1), is_transpose=True)
+            mag = sb.tile([P, P], F32, name="mag_%d" % h)
+            root = sb.tile([P, P], F32, name="root_%d" % h)
+            inv_t = sb.tile([P, P], F32, name="inv_t_%d" % h)
+            nc.scalar.activation(out=mag[:], in_=sums[:], func=ACT.Abs, scale=1.0 / GROUP)
+            nc.scalar.activation(out=root[:], in_=mag[:], func=ACT.Abs_reciprocal_sqrt, bias=one[:])
+            nc.scalar.activation(out=inv_t[:], in_=root[:], func=ACT.Square)
+            nc.tensor.transpose(inv[:, h, :], inv_t[:], ident[:])
+
+        hi = sb.tile([P, HALVES, W], F32, name="hi")
+        lo = sb.tile([P, HALVES, W], F32, name="lo")
+        span = sb.tile([P, HALVES, W], F32, name="span")
+        nc.vector.tensor_tensor(out=hi[:], in0=hi2[:, :, 0, :], in1=hi2[:, :, 1, :], op=ALU.max)
+        nc.vector.tensor_tensor(out=lo[:], in0=lo2[:, :, 0, :], in1=lo2[:, :, 1, :], op=ALU.min)
+        nc.vector.tensor_tensor(out=span[:], in0=hi[:], in1=lo[:], op=ALU.subtract)
+
+        y = sb.tile([P, PACK, B], F32, name="y")
+        y_bf = sb.tile([P, B, PACK], BF16, name="y_bf", align_bytes=64)
+        nc.vector.tensor_tensor(
+            out=y_bf[:].rearrange("p (h b) t -> p h b t", h=HALVES),
+            in0=span[:].rearrange("p h (t b) -> p h b t", t=PACK),
+            in1=inv[:].rearrange("p h (t b) -> p h b t", t=PACK),
+            op=ALU.mult,
+        )
+        nc.vector.tensor_tensor(
+            out=y[:].rearrange("p t (h b) -> p h t b", h=HALVES),
+            in0=span[:].rearrange("p h (t b) -> p h t b", t=PACK),
+            in1=inv[:].rearrange("p h (t b) -> p h t b", t=PACK),
+            op=ALU.mult,
+        )
+        y_codes = sb.tile([P, B], U32, name="y_codes", align_bytes=64)
+        y_scales = sb.tile([P, B], U8, name="y_scales", align_bytes=64)
+        nc.vector.quantize_mx(out=y_codes[:].bitcast(FP8X4), scales=y_scales[:], in_=y_bf[:].rearrange("p b t -> p (b t)"))
+
+        nc.sync.dma_start(out=out_0.rearrange("(p t) b -> p (t b)", t=PACK), in_=y[:].rearrange("p t b -> p (t b)"))
+        nc.scalar.dma_start(out=out_1[0].rearrange("p c r -> p (c r)").bitcast(I32), in_=y_codes[:].bitcast(I32))
+        for q in range(4):
+            queue = nc.sync if q % 2 == 0 else nc.scalar
+            queue.dma_start(out=out_2[0, 4 * q : 4 * q + 4, :].bitcast(I32), in_=y_scales[32 * q : 32 * q + 4, :].bitcast(I32))

@@ -25,8 +25,10 @@ HALVES = 2
 JH = J // HALVES
 BH = B // HALVES
 NMM = 128
-PAIRS = 2
-TP = PACK // PAIRS
+SIDES = 2
+IS = GROUP // SIDES
+WOVEN = [4, 2]
+LOAD_ORDER = [(1, 0), (1, 1), (0, 0), (0, 1), (0, 2), (0, 3), (1, 2), (1, 3)]
 
 
 def tile_list_range_of_picked_groups_pl_kernel(tc, xt, w_words, w_scales, offs, out_0, out_1, out_2):
@@ -48,8 +50,8 @@ def tile_list_range_of_picked_groups_pl_kernel(tc, xt, w_words, w_scales, offs, 
             )
         rows = xt.rearrange("(a p t) c -> a t p c", a=PASSES, t=PACK)
         planes = {}
-        for a in range(PASSES):
-            for t in range(PACK):
+        for a, t in LOAD_ORDER:
+            if True:
                 planes[a, t] = sb.tile([P, T], F32, name="plane_%d_%d" % (a, t))
                 nc.sync.dma_start(out=planes[a, t][:], in_=rows[a, t])
 
@@ -63,8 +65,8 @@ def tile_list_range_of_picked_groups_pl_kernel(tc, xt, w_words, w_scales, offs, 
         w_dealt = sb.tile([P, PASSES * PACK, 2 * P], U8, name="w_dealt", align_bytes=64)
         ws_dealt = sb.tile([P, PASSES * PACK, P], U8, name="ws_dealt", align_bytes=64)
         nc.vector.tensor_copy(
-            out=w_dealt[:].rearrange("p (a t) (q two) -> p a t q two", t=PACK, two=2),
-            in_=w_raw[:].rearrange("p a (q t two) -> p a t q two", t=PACK, two=2),
+            out=w_dealt[:].bitcast(U16).rearrange("p (a t) q -> p a t q", t=PACK),
+            in_=w_raw[:].bitcast(U16).rearrange("p a (q t) -> p a t q", t=PACK),
         )
         nc.vector.tensor_copy(
             out=ws_dealt[:].rearrange("p (a t) q -> p a t q", t=PACK),
@@ -72,99 +74,120 @@ def tile_list_range_of_picked_groups_pl_kernel(tc, xt, w_words, w_scales, offs, 
         )
 
         banks = {}
+        picked = {}
+        dense = {}
         for h in range(HALVES):
-            for u in range(PAIRS):
-                banks[h, u] = ps.tile([P, TP, JH], F32, name="z_%d_%d" % (h, u))
+            for v in range(SIDES):
+                banks[h, v] = ps.tile([P, PACK, NMM], F32, name="z_%d_%d" % (h, v))
+            for a in range(PASSES):
+                picked[a, h] = sb.tile([P, JH, PACK], BF16, name="picked_%d_%d" % (a, h), align_bytes=64)
+                dense[a, h] = sb.tile([P, WOVEN[a], JH], F32, name="dense_%d_%d" % (a, h))
 
-        def gather(a, t, h, picked):
-            nc.vector.tensor_copy(
-                out=picked[:, :, t],
-                in_=planes[a, t][:].indirect(offsets[:, h * (JH // 16) : (h + 1) * (JH // 16)]),
-            )
+        def window(a, t, h):
+            return planes[a, t][:].indirect(offsets[:, h * (JH // 16) : (h + 1) * (JH // 16)])
 
-        def multiply(a, h, picked):
+        def gather(a, t, h):
+            if t < WOVEN[a]:
+                nc.vector.tensor_copy(out=dense[a, h][:, t, :], in_=window(a, t, h))
+            else:
+                nc.vector.tensor_copy(
+                    out=picked[a, h][:, :, t].rearrange("p (v b i) -> p b v i", v=SIDES, i=IS),
+                    in_=window(a, t, h),
+                )
+            if t == WOVEN[a] - 1:
+                nc.scalar.copy(
+                    out=picked[a, h][:, :, 0 : WOVEN[a]].rearrange("p (v b i) t -> p v b t i", v=SIDES, i=IS),
+                    in_=dense[a, h][:].rearrange("p t (b v i) -> p v b t i", v=SIDES, i=IS),
+                )
+
+        def multiply(a, h):
             codes = sb.tile([P, JH], U32, name="codes_%d_%d" % (a, h), align_bytes=64)
             scales = sb.tile([P, JH], U8, name="scales_%d_%d" % (a, h), align_bytes=64)
-            nc.vector.quantize_mx(out=codes[:].bitcast(FP8X4), scales=scales[:], in_=picked[:].rearrange("p j t -> p (j t)"))
-            for u in range(PAIRS):
-                for t2 in range(TP):
-                    s = a * PACK + u * TP + t2
-                    for c in range(JH // NMM):
-                        cols = slice(c * NMM, (c + 1) * NMM)
-                        nc.tensor.matmul_mx(
-                            out=banks[h, u][:, t2, cols],
-                            lhsT=w_dealt[:, s, :].bitcast(FP4X4),
-                            lhsT_scale=ws_dealt[:, s, :],
-                            rhs=codes[:, cols].bitcast(FP8X4),
-                            rhs_scale=scales[:, cols],
-                            start=(a == 0 and t2 == 0 and c == 0),
-                            stop=(a == PASSES - 1 and t2 == TP - 1 and c == JH // NMM - 1),
-                        )
+            nc.vector.quantize_mx(out=codes[:].bitcast(FP8X4), scales=scales[:], in_=picked[a, h][:].rearrange("p j t -> p (j t)"))
+            for v in range(SIDES):
+                cols = slice(v * NMM, (v + 1) * NMM)
+                for t in range(PACK):
+                    nc.tensor.matmul_mx(
+                        out=banks[h, v][:, t, :],
+                        lhsT=w_dealt[:, a * PACK + t, :].bitcast(FP4X4),
+                        lhsT_scale=ws_dealt[:, a * PACK + t, :],
+                        rhs=codes[:, cols].bitcast(FP8X4),
+                        rhs_scale=scales[:, cols],
+                        start=(a == 0 and t == 0),
+                        stop=(a == PASSES - 1 and t == PACK - 1),
+                    )
 
-        for a in range(PASSES):
-            picked = [sb.tile([P, JH, PACK], BF16, name="picked_%d_%d" % (a, h), align_bytes=64) for h in range(HALVES)]
-            for t in range(PACK):
-                for h in range(HALVES):
-                    gather(a, t, h, picked[h])
-                    if t == PACK - 1:
-                        multiply(a, h, picked[h])
+        for a, t in LOAD_ORDER:
+            for h in range(HALVES):
+                gather(a, t, h)
+                if t == PACK - 1:
+                    multiply(a, h)
 
-        W = PACK * BH
-        hi4 = sb.tile([P, HALVES, 4, W], F32, name="hi4")
-        lo4 = sb.tile([P, HALVES, 4, W], F32, name="lo4")
-        hi2 = sb.tile([P, HALVES, 2, W], F32, name="hi2")
-        lo2 = sb.tile([P, HALVES, 2, W], F32, name="lo2")
-        inv = ps.tile([P, HALVES, W], F32, name="inv")
-        for h in range(HALVES):
-            z = sb.tile([P, GROUP, W], F32, name="zs_%d" % h)
-            for u in range(PAIRS):
-                cols = slice(u * TP * BH, (u + 1) * TP * BH)
-                nc.scalar.copy(
-                    out=z[:, :, cols].rearrange("p i (t b) -> p i t b", t=TP),
-                    in_=banks[h, u][:].rearrange("p t (b i) -> p i t b", i=GROUP),
-                )
-                nc.vector.tensor_tensor(out=hi4[:, h, :, cols], in0=z[:, 0:4, cols], in1=z[:, 4:8, cols], op=ALU.max)
-                nc.vector.tensor_tensor(out=lo4[:, h, :, cols], in0=z[:, 0:4, cols], in1=z[:, 4:8, cols], op=ALU.min)
-            nc.vector.tensor_tensor(out=hi2[:, h], in0=hi4[:, h, 0:2, :], in1=hi4[:, h, 2:4, :], op=ALU.max)
-            nc.vector.tensor_tensor(out=lo2[:, h], in0=lo4[:, h, 0:2, :], in1=lo4[:, h, 2:4, :], op=ALU.min)
-            sums = ps.tile([P, P], F32, name="sums_%d" % h)
-            for i in range(GROUP):
-                nc.tensor.matmul(sums[:], lhsT=z[:, i, :], rhs=ident[:], start=(i == 0), stop=(i == GROUP - 1), is_transpose=True)
+        W = BH * PACK
+        y = sb.tile([P, PACK, B], F32, name="y")
+        y_bf = sb.tile([P, B * PACK], BF16, name="y_bf", align_bytes=64)
+        z = [sb.tile([P, GROUP, W], F32, name="zs_%d" % h) for h in range(HALVES)]
+        hi4 = [sb.tile([P, SIDES, 2, W], F32, name="hi4_%d" % h) for h in range(HALVES)]
+        lo4 = [sb.tile([P, SIDES, 2, W], F32, name="lo4_%d" % h) for h in range(HALVES)]
+        sums = [ps.tile([P, W], F32, name="sums_%d" % h) for h in range(HALVES)]
+        inv = [ps.tile([P, W], F32, name="inv_%d" % h) for h in range(HALVES)]
+        span = [sb.tile([P, W], F32, name="span_%d" % h) for h in range(HALVES)]
+
+        def drain(h, v):
+            zv = z[h][:, v * IS : (v + 1) * IS, :]
+            nc.scalar.copy(
+                out=zv.rearrange("p i (b t) -> p i b t", t=PACK),
+                in_=banks[h, v][:].rearrange("p t (b i) -> p i b t", i=IS),
+            )
+            nc.vector.tensor_tensor(out=hi4[h][:, v], in0=zv[:, 0:2, :], in1=zv[:, 2:4, :], op=ALU.max)
+            nc.vector.tensor_tensor(out=lo4[h][:, v], in0=zv[:, 0:2, :], in1=zv[:, 2:4, :], op=ALU.min)
+            for i in range(v * IS, (v + 1) * IS):
+                nc.tensor.matmul(sums[h][:], lhsT=z[h][:, i, :], rhs=ident[:], start=(i == 0), stop=(i == GROUP - 1), is_transpose=True)
+
+        def spread(h):
+            hi2 = sb.tile([P, 2, W], F32, name="hi2_%d" % h)
+            lo2 = sb.tile([P, 2, W], F32, name="lo2_%d" % h)
+            hi = sb.tile([P, W], F32, name="hi_%d" % h)
+            lo = sb.tile([P, W], F32, name="lo_%d" % h)
+            nc.vector.tensor_tensor(out=hi2[:], in0=hi4[h][:, 0], in1=hi4[h][:, 1], op=ALU.max)
+            nc.vector.tensor_tensor(out=lo2[:], in0=lo4[h][:, 0], in1=lo4[h][:, 1], op=ALU.min)
+            nc.vector.tensor_tensor(out=hi[:], in0=hi2[:, 0], in1=hi2[:, 1], op=ALU.max)
+            nc.vector.tensor_tensor(out=lo[:], in0=lo2[:, 0], in1=lo2[:, 1], op=ALU.min)
+            nc.vector.tensor_tensor(out=span[h][:], in0=hi[:], in1=lo[:], op=ALU.subtract)
+
+        def invert(h):
             mag = sb.tile([P, P], F32, name="mag_%d" % h)
             root = sb.tile([P, P], F32, name="root_%d" % h)
             inv_t = sb.tile([P, P], F32, name="inv_t_%d" % h)
-            nc.scalar.activation(out=mag[:], in_=sums[:], func=ACT.Abs, scale=1.0 / GROUP)
+            nc.scalar.activation(out=mag[:], in_=sums[h][:], func=ACT.Abs, scale=1.0 / GROUP)
             nc.scalar.activation(out=root[:], in_=mag[:], func=ACT.Abs_reciprocal_sqrt, bias=one[:])
             nc.scalar.activation(out=inv_t[:], in_=root[:], func=ACT.Square)
-            nc.tensor.transpose(inv[:, h, :], inv_t[:], ident[:])
+            nc.tensor.transpose(inv[h][:], inv_t[:], ident[:])
 
-        hi = sb.tile([P, HALVES, W], F32, name="hi")
-        lo = sb.tile([P, HALVES, W], F32, name="lo")
-        span = sb.tile([P, HALVES, W], F32, name="span")
-        nc.vector.tensor_tensor(out=hi[:], in0=hi2[:, :, 0, :], in1=hi2[:, :, 1, :], op=ALU.max)
-        nc.vector.tensor_tensor(out=lo[:], in0=lo2[:, :, 0, :], in1=lo2[:, :, 1, :], op=ALU.min)
-        nc.vector.tensor_tensor(out=span[:], in0=hi[:], in1=lo[:], op=ALU.subtract)
+        def finish(h):
+            nc.vector.tensor_tensor(out=y_bf[:, h * W : (h + 1) * W], in0=span[h][:], in1=inv[h][:], op=ALU.mult)
+            nc.vector.tensor_tensor(
+                out=y[:, :, h * BH : (h + 1) * BH].rearrange("p t (c i) -> p c t i", i=4),
+                in0=span[h][:].rearrange("p (c i t) -> p c t i", i=4, t=PACK),
+                in1=inv[h][:].rearrange("p (c i t) -> p c t i", i=4, t=PACK),
+                op=ALU.mult,
+            )
 
-        y = sb.tile([P, PACK, B], F32, name="y")
-        y_bf = sb.tile([P, B, PACK], BF16, name="y_bf", align_bytes=64)
-        nc.vector.tensor_tensor(
-            out=y_bf[:].rearrange("p (h b) t -> p h b t", h=HALVES),
-            in0=span[:].rearrange("p h (t b) -> p h b t", t=PACK),
-            in1=inv[:].rearrange("p h (t b) -> p h b t", t=PACK),
-            op=ALU.mult,
-        )
-        nc.vector.tensor_tensor(
-            out=y[:].rearrange("p t (h b) -> p h t b", h=HALVES),
-            in0=span[:].rearrange("p h (t b) -> p h t b", t=PACK),
-            in1=inv[:].rearrange("p h (t b) -> p h t b", t=PACK),
-            op=ALU.mult,
-        )
+        for h in range(HALVES):
+            for v in range(SIDES):
+                drain(h, v)
+        for h in range(HALVES):
+            invert(h)
+            spread(h)
+        for h in range(HALVES):
+            finish(h)
+
         y_codes = sb.tile([P, B], U32, name="y_codes", align_bytes=64)
         y_scales = sb.tile([P, B], U8, name="y_scales", align_bytes=64)
-        nc.vector.quantize_mx(out=y_codes[:].bitcast(FP8X4), scales=y_scales[:], in_=y_bf[:].rearrange("p b t -> p (b t)"))
+        nc.vector.quantize_mx(out=y_codes[:].bitcast(FP8X4), scales=y_scales[:], in_=y_bf[:])
 
         nc.sync.dma_start(out=out_0.rearrange("(p t) b -> p (t b)", t=PACK), in_=y[:].rearrange("p t b -> p (t b)"))
-        nc.scalar.dma_start(out=out_1[0].rearrange("p c r -> p (c r)").bitcast(I32), in_=y_codes[:].bitcast(I32))
+        nc.sync.dma_start(out=out_1[0].rearrange("p c r -> p (c r)").bitcast(I32), in_=y_codes[:].bitcast(I32))
         for q in range(4):
-            queue = nc.sync if q % 2 == 0 else nc.scalar
+            queue = nc.sync if q == 0 else nc.scalar
             queue.dma_start(out=out_2[0, 4 * q : 4 * q + 4, :].bitcast(I32), in_=y_scales[32 * q : 32 * q + 4, :].bitcast(I32))

from contextlib import ExitStack

import concourse.mybir as mybir
from concourse.masks import make_identity

K, T, J, B, N = 1024, 2048, 512, 64, 512
FLOPS = 2 * K * J * N

F32 = mybir.dt.float32
BF16 = mybir.dt.bfloat16
I32 = mybir.dt.int32
U32 = mybir.dt.uint32
U16 = mybir.dt.uint16
U8 = mybir.dt.uint8
FP8X4 = mybir.dt.float8_e4m3fn_x4
FP4X4 = mybir.dt.float4_e2m1fn_x4
ALU = mybir.AluOpType
ACT = mybir.ActivationFunctionType

P = 128
PACK = 4
PASSES = K // (P * PACK)
GROUP = J // B
HALVES = 2
JH = J // HALVES
BH = B // HALVES
NMM = 128
SIDES = 2
IS = GROUP // SIDES
WOVEN = [4, 2]
LOAD_ORDER = [(1, 0), (1, 1), (0, 0), (0, 1), (0, 2), (0, 3), (1, 2), (1, 3)]


def tile_list_range_of_picked_groups_pl_kernel(tc, xt, w_words, w_scales, offs, out_0, out_1, out_2):
    nc = tc.nc
    with ExitStack() as ctx:
        sb = ctx.enter_context(tc.tile_pool(name="sb", bufs=1))
        ps = ctx.enter_context(tc.psum_pool(name="ps", bufs=1))

        offsets = sb.tile([P, J // 16], U16, name="offsets")
        w_raw = sb.tile([P, PASSES, 2 * N], U8, name="w_raw")
        ws_raw = sb.tile([P, PASSES, N], U8, name="ws_raw")
        nc.vector.memset(ws_raw[:].bitcast(I32), 0)
        nc.sync.dma_start(out=w_raw[:].bitcast(I32), in_=w_words.rearrange("a p c -> p a c").bitcast(I32))
        nc.sync.dma_start(offsets[:], offs)
        for q in range(4):
            nc.scalar.dma_start(
                out=ws_raw[32 * q : 32 * q + 4, :, :].bitcast(I32),
                in_=w_scales[:, 4 * q : 4 * q + 4, :].rearrange("a r c -> r a c").bitcast(I32),
            )
        rows = xt.rearrange("(a p t) c -> a t p c", a=PASSES, t=PACK)
        planes = {}
        for a, t in LOAD_ORDER:
            if True:
                planes[a, t] = sb.tile([P, T], F32, name="plane_%d_%d" % (a, t))
                nc.sync.dma_start(out=planes[a, t][:], in_=rows[a, t])

        one = sb.tile([P, 1], F32, name="one")
        nc.gpsimd.memset(one[:], 1.0)
        warm = sb.tile([P, 1], F32, name="warm")
        nc.scalar.activation(out=warm[:], in_=one[:], func=ACT.Abs_reciprocal_sqrt, bias=one[:])
        ident = sb.tile([P, P], F32, name="ident")
        make_identity(nc, ident[:])

        w_dealt = sb.tile([P, PASSES * PACK, 2 * P], U8, name="w_dealt", align_bytes=64)
        ws_dealt = sb.tile([P, PASSES * PACK, P], U8, name="ws_dealt", align_bytes=64)
        nc.vector.tensor_copy(
            out=w_dealt[:].bitcast(U16).rearrange("p (a t) q -> p a t q", t=PACK),
            in_=w_raw[:].bitcast(U16).rearrange("p a (q t) -> p a t q", t=PACK),
        )
        nc.vector.tensor_copy(
            out=ws_dealt[:].rearrange("p (a t) q -> p a t q", t=PACK),
            in_=ws_raw[:].rearrange("p a (q t) -> p a t q", t=PACK),
        )

        banks = {}
        picked = {}
        dense = {}
        for h in range(HALVES):
            for v in range(SIDES):
                banks[h, v] = ps.tile([P, PACK, NMM], F32, name="z_%d_%d" % (h, v))
            for a in range(PASSES):
                picked[a, h] = sb.tile([P, JH, PACK], BF16, name="picked_%d_%d" % (a, h), align_bytes=64)
                dense[a, h] = sb.tile([P, WOVEN[a], JH], F32, name="dense_%d_%d" % (a, h))

        def window(a, t, h):
            return planes[a, t][:].indirect(offsets[:, h * (JH // 16) : (h + 1) * (JH // 16)])

        def gather(a, t, h):
            if t < WOVEN[a]:
                nc.vector.tensor_copy(out=dense[a, h][:, t, :], in_=window(a, t, h))
            else:
                nc.vector.tensor_copy(
                    out=picked[a, h][:, :, t].rearrange("p (v b i) -> p b v i", v=SIDES, i=IS),
                    in_=window(a, t, h),
                )
            if t == WOVEN[a] - 1:
                nc.scalar.copy(
                    out=picked[a, h][:, :, 0 : WOVEN[a]].rearrange("p (v b i) t -> p v b t i", v=SIDES, i=IS),
                    in_=dense[a, h][:].rearrange("p t (b v i) -> p v b t i", v=SIDES, i=IS),
                )

        def multiply(a, h):
            codes = sb.tile([P, JH], U32, name="codes_%d_%d" % (a, h), align_bytes=64)
            scales = sb.tile([P, JH], U8, name="scales_%d_%d" % (a, h), align_bytes=64)
            nc.vector.quantize_mx(out=codes[:].bitcast(FP8X4), scales=scales[:], in_=picked[a, h][:].rearrange("p j t -> p (j t)"))
            for v in range(SIDES):
                cols = slice(v * NMM, (v + 1) * NMM)
                for t in range(PACK):
                    nc.tensor.matmul_mx(
                        out=banks[h, v][:, t, :],
                        lhsT=w_dealt[:, a * PACK + t, :].bitcast(FP4X4),
                        lhsT_scale=ws_dealt[:, a * PACK + t, :],
                        rhs=codes[:, cols].bitcast(FP8X4),
                        rhs_scale=scales[:, cols],
                        start=(a == 0 and t == 0),
                        stop=(a == PASSES - 1 and t == PACK - 1),
                    )

        for a, t in LOAD_ORDER:
            for h in range(HALVES):
                gather(a, t, h)
                if t == PACK - 1:
                    multiply(a, h)

        W = BH * PACK
        y = sb.tile([P, PACK, B], F32, name="y")
        y_bf = sb.tile([P, B * PACK], BF16, name="y_bf", align_bytes=64)
        z = [sb.tile([P, GROUP, W], F32, name="zs_%d" % h) for h in range(HALVES)]
        hi4 = [sb.tile([P, SIDES, 2, W], F32, name="hi4_%d" % h) for h in range(HALVES)]
        lo4 = [sb.tile([P, SIDES, 2, W], F32, name="lo4_%d" % h) for h in range(HALVES)]
        sums = [ps.tile([P, W], F32, name="sums_%d" % h) for h in range(HALVES)]
        inv = [ps.tile([P, W], F32, name="inv_%d" % h) for h in range(HALVES)]
        span = [sb.tile([P, W], F32, name="span_%d" % h) for h in range(HALVES)]

        def drain(h, v):
            zv = z[h][:, v * IS : (v + 1) * IS, :]
            nc.scalar.copy(
                out=zv.rearrange("p i (b t) -> p i b t", t=PACK),
                in_=banks[h, v][:].rearrange("p t (b i) -> p i b t", i=IS),
            )
            nc.vector.tensor_tensor(out=hi4[h][:, v], in0=zv[:, 0:2, :], in1=zv[:, 2:4, :], op=ALU.max)
            nc.vector.tensor_tensor(out=lo4[h][:, v], in0=zv[:, 0:2, :], in1=zv[:, 2:4, :], op=ALU.min)
            for i in range(v * IS, (v + 1) * IS):
                nc.tensor.matmul(sums[h][:], lhsT=z[h][:, i, :], rhs=ident[:], start=(i == 0), stop=(i == GROUP - 1), is_transpose=True)

        def spread(h):
            hi2 = sb.tile([P, 2, W], F32, name="hi2_%d" % h)
            lo2 = sb.tile([P, 2, W], F32, name="lo2_%d" % h)
            hi = sb.tile([P, W], F32, name="hi_%d" % h)
            lo = sb.tile([P, W], F32, name="lo_%d" % h)
            nc.vector.tensor_tensor(out=hi2[:], in0=hi4[h][:, 0], in1=hi4[h][:, 1], op=ALU.max)
            nc.vector.tensor_tensor(out=lo2[:], in0=lo4[h][:, 0], in1=lo4[h][:, 1], op=ALU.min)
            nc.vector.tensor_tensor(out=hi[:], in0=hi2[:, 0], in1=hi2[:, 1], op=ALU.max)
            nc.vector.tensor_tensor(out=lo[:], in0=lo2[:, 0], in1=lo2[:, 1], op=ALU.min)
            nc.vector.tensor_tensor(out=span[h][:], in0=hi[:], in1=lo[:], op=ALU.subtract)

        def invert(h):
            mag = sb.tile([P, P], F32, name="mag_%d" % h)
            root = sb.tile([P, P], F32, name="root_%d" % h)
            inv_t = sb.tile([P, P], F32, name="inv_t_%d" % h)
            nc.scalar.activation(out=mag[:], in_=sums[h][:], func=ACT.Abs, scale=1.0 / GROUP)
            nc.scalar.activation(out=root[:], in_=mag[:], func=ACT.Abs_reciprocal_sqrt, bias=one[:])
            nc.scalar.activation(out=inv_t[:], in_=root[:], func=ACT.Square)
            nc.tensor.transpose(inv[h][:], inv_t[:], ident[:])

        def finish(h):
            nc.vector.tensor_tensor(out=y_bf[:, h * W : (h + 1) * W], in0=span[h][:], in1=inv[h][:], op=ALU.mult)
            nc.vector.tensor_tensor(
                out=y[:, :, h * BH : (h + 1) * BH].rearrange("p t (c i) -> p c t i", i=4),
                in0=span[h][:].rearrange("p (c i t) -> p c t i", i=4, t=PACK),
                in1=inv[h][:].rearrange("p (c i t) -> p c t i", i=4, t=PACK),
                op=ALU.mult,
            )

        for h in range(HALVES):
            for v in range(SIDES):
                drain(h, v)
        for h in range(HALVES):
            invert(h)
            spread(h)
        for h in range(HALVES):
            finish(h)

        y_codes = sb.tile([P, B], U32, name="y_codes", align_bytes=64)
        y_scales = sb.tile([P, B], U8, name="y_scales", align_bytes=64)
        nc.vector.quantize_mx(out=y_codes[:].bitcast(FP8X4), scales=y_scales[:], in_=y_bf[:])

        nc.sync.dma_start(out=out_0.rearrange("(p t) b -> p (t b)", t=PACK), in_=y[:].rearrange("p t b -> p (t b)"))
        nc.sync.dma_start(out=out_1[0].rearrange("p c r -> p (c r)").bitcast(I32), in_=y_codes[:].bitcast(I32))
        for q in range(4):
            queue = nc.sync if q == 0 else nc.scalar
            queue.dma_start(out=out_2[0, 4 * q : 4 * q + 4, :].bitcast(I32), in_=y_scales[32 * q : 32 * q + 4, :].bitcast(I32))
